import numpy as np
import ml_dtypes


def mxq(x, axis, fmt="e4m3"):
    dtype, down = {"e4m3": (ml_dtypes.float8_e4m3fn, 7), "e5m2": (ml_dtypes.float8_e5m2, 14)}[fmt]
    v = np.moveaxis(np.asarray(x, np.float32).astype(ml_dtypes.bfloat16).astype(np.float64), axis, -1)
    blocks = v.reshape(v.shape[:-1] + (-1, 32))
    amax = np.abs(blocks).max(-1, keepdims=True)
    byte = np.maximum(np.where(amax > 0, np.frexp(amax)[1] - 1 + 127, 0) - down, 1)
    scale = np.exp2(byte - 127.0)
    codes = (blocks / scale).astype(np.float32).astype(dtype).astype(np.float64)
    return np.moveaxis((codes * scale).reshape(v.shape), -1, axis)


WIDE = False


def mx_kscale(k):
    if not WIDE:
        return np.ones(k)
    levels = np.array([10, -10, 5, -5, 0])
    if k % 512:
        return np.exp2(np.random.permutation(np.resize(levels, k // 32))).repeat(32)
    a = np.empty((k // 512, 16))
    for p in range(k // 512):
        a[p, :8] = np.random.permutation(np.resize(levels, 8))
        for g in range(8):
            far = levels[np.abs(levels - a[p, g]) >= 10]
            a[p, g + 8] = far[np.random.randint(len(far))]
    return np.exp2(a.ravel()).repeat(32)


def f64(x):
    return np.asarray(x).astype(np.float64)


def striped(idx):
    return np.tile(idx.reshape(-1, 16).T, (8, 1)).astype(np.uint16)


def unstriped(offs):
    return offs[:16].T.reshape(-1).astype(np.int64)


def striped8(idx):
    return np.concatenate([x.reshape(-1, 16).T for x in idx]).astype(np.uint16)


def runs(offs, k):
    lists = np.stack([offs[16 * r : 16 * r + 16].T.reshape(-1) for r in range(8)]).astype(np.int64)
    return lists[np.arange(k) % 512 // 64]


def pack_weight(w):
    k, n = w.shape
    w = f64(np.asarray(w, np.float32).astype(ml_dtypes.bfloat16)).reshape(k // 32, 32, n)
    amax = np.abs(w).max(1)
    byte = np.clip(np.where(amax > 0, np.frexp(amax)[1] - 1 + 127 - 7, 1), 1, 254)
    scaled = (w * np.exp2(127.0 - byte)[:, None, :]).reshape(k, n).astype(np.float32)
    words = np.ascontiguousarray(scaled.reshape(k // 512, 128, 4, n).transpose(0, 1, 3, 2)).astype(ml_dtypes.float8_e4m3fn).view(np.uint8)
    return words, np.ascontiguousarray(byte.astype(np.uint8).reshape(k // 512, 16, n))


def unpack_weight(words, scales):
    g, p, n, _ = words.shape
    vals = np.ascontiguousarray(words).view(ml_dtypes.float8_e4m3fn).astype(np.float64) * np.repeat(np.exp2(scales.astype(np.float64) - 127.0), 8, axis=1)[..., None]
    return vals.transpose(0, 1, 3, 2).reshape(g * 512, n)


E2M1 = np.array([0.0, 0.5, 1.0, 1.5, 2.0, 3.0, 4.0, 6.0, -0.0, -0.5, -1.0, -1.5, -2.0, -3.0, -4.0, -6.0])


def pack_fp4(w):
    k, n = w.shape
    w = f64(np.asarray(w, np.float32).astype(ml_dtypes.bfloat16)).reshape(k // 32, 32, n)
    amax = np.abs(w).max(1)
    mant, ex = np.frexp(amax / 6.0)
    byte = np.clip(np.where(amax > 0, np.where(mant > 0.5, ex, ex - 1) + 127, 1), 1, 254)
    scaled = (w * np.exp2(127.0 - byte)[:, None, :]).reshape(k, n).astype(np.float32)
    c = np.ascontiguousarray(scaled.reshape(k // 512, 128, 4, n).transpose(0, 1, 3, 2)).astype(ml_dtypes.float4_e2m1fn).view(np.uint8) & 0xF
    words = (c[..., 0::2] | (c[..., 1::2] << 4)).reshape(k // 512, 128, 2 * n)
    return np.ascontiguousarray(words), np.ascontiguousarray(byte.astype(np.uint8).reshape(k // 512, 16, n))


def unpack_fp4(words, scales):
    g, _, n = scales.shape
    words = np.ascontiguousarray(words).reshape(g, 128, n, 2)
    nib = np.empty((g, 128, n, 4), np.uint8)
    nib[..., 0::2] = words & 0xF
    nib[..., 1::2] = words >> 4
    vals = E2M1[nib] * np.repeat(np.exp2(scales.astype(np.float64) - 127.0), 8, axis=1)[..., None]
    return vals.transpose(0, 1, 3, 2).reshape(g * 512, n)


def sigmoid(v):
    return 1.0 / (1.0 + np.exp(-np.maximum(v, -700.0)))

def planes(y):
    n, m = y.shape
    v = y.astype(np.float32).astype(ml_dtypes.bfloat16).astype(np.float64).reshape(n // 32, 32, m)
    top = np.abs(v).max(1)
    byte = np.clip(np.where(top > 0, np.frexp(top)[1] - 1 + 127 - 7, 1), 1, 254)
    codes = (v * np.exp2(127.0 - byte)[:, None, :]).reshape(n, m).astype(np.float32).astype(ml_dtypes.float8_e4m3fn).view(np.uint8)
    words = codes.reshape(n // 512, 128, 4, m).transpose(0, 1, 3, 2)
    return np.ascontiguousarray(words), np.ascontiguousarray(byte.astype(np.uint8).reshape(n // 512, 16, m))


K, T, S, V, H, J = 512, 2048, 512, 512, 512, 512


def setup_inputs():
    n = np.random.standard_normal
    s = mx_kscale(K)[:, None]
    u = mx_kscale(S)
    packed_xT = pack_weight(n((K, T)) * s)
    packed_w1 = pack_fp4(n((K, H)) / np.sqrt(K) / s)
    packed_w2 = pack_fp4(n((K, H)) / np.sqrt(K) / s)
    return {
        "x_words": packed_xT[0],
        "x_scales": packed_xT[1],
        "w1_words": packed_w1[0],
        "w1_scales": packed_w1[1],
        "w2_words": packed_w2[0],
        "w2_scales": packed_w2[1],
        "tab": np.random.uniform(0.4, 1.4, (H, J)).astype(np.float32),
        "ga": (np.random.uniform(0.5, 1.5, (H, 1)) * u[:, None]).astype(np.float32),
        "gb": (np.random.uniform(0.5, 1.5, (H, 1)) / u[:, None]).astype(np.float32),
        "offs": striped8(np.random.randint(0, T, (8, S))),
        "two": striped(np.random.permutation(T)[:V]),
        "n1": striped8(np.stack([np.random.permutation(S) for _ in range(8)])),
        "n2": striped8(np.random.randint(0, J, (8, V))),
        "n3": striped8(np.stack([np.random.permutation(V) for _ in range(8)])),
        "n4": striped8(np.stack([np.random.permutation(V) for _ in range(8)])),
        "n5": striped8(np.stack([np.random.permutation(V) for _ in range(8)])),
    }


def reference(x_words, x_scales, w1_words, w1_scales, w2_words, w2_scales, tab, ga, gb, offs, two, n1, n2, n3, n4, n5):
    xq = unpack_weight(x_words, x_scales)[np.arange(K)[:, None], runs(offs, K)]
    a = unpack_fp4(w1_words, w1_scales).T @ xq
    st = a * (sigmoid(a[np.arange(H)[:, None], runs(n1, H)]))
    z = f64(ga) * (np.maximum(st, st[np.arange(H)[:, None], runs(n1, H)]))
    x_two = unpack_weight(x_words, x_scales)[:, unstriped(two)]
    b = unpack_fp4(w2_words, w2_scales).T @ x_two
    z2 = f64(gb) * (b * (f64(tab)[np.arange(H)[:, None], runs(n2, H)]) - (0.5 * (b[np.arange(H)[:, None], runs(n3, H)])))
    s = 0.0625 * ((mxq(z, 0, "e4m3").T @ mxq(z2, 0, "e4m3")))
    out_0 = np.maximum(s[np.arange(S)[:, None], runs(n4, S)], s[np.arange(S)[:, None], runs(n5, S)]) - (0.75 * s)
    return (out_0,) + planes(out_0)

@@ -1,0 +1,253 @@
+from contextlib import ExitStack
+
+import concourse.mybir as mybir
+
+F32 = mybir.dt.float32
+BF16 = mybir.dt.bfloat16
+I32 = mybir.dt.int32
+U32 = mybir.dt.uint32
+U16 = mybir.dt.uint16
+U8 = mybir.dt.uint8
+FP8X4 = mybir.dt.float8_e4m3fn_x4
+FP4X4 = mybir.dt.float4_e2m1fn_x4
+ALU = mybir.AluOpType
+ACT = mybir.ActivationFunctionType
+
+P = 128
+R = 4
+N = 512
+T = 2048
+HALF = 256
+FLOPS = 3 * 2 * 512 * 512 * 512
+
+
+def tile_picked_hkqtwicpkindgover_none_po_kernel(
+    tc, x_words, x_scales, w1_words, w1_scales, w2_words, w2_scales, tab, ga, gb,
+    offs, two, n1, n2, n3, n4, n5, out_0, out_1, out_2,
+):
+    nc = tc.nc
+    with ExitStack() as ctx:
+        keep = ctx.enter_context(tc.tile_pool(name="keep", bufs=1))
+        psum = ctx.enter_context(tc.psum_pool(name="psum", bufs=1))
+
+        def sb(name, shape, dtype):
+            return keep.tile(shape, dtype, name=name, align_bytes=64)
+
+        def planes(name, width):
+            return [sb("%s%d" % (name, t), [P, width], F32) for t in range(R)]
+
+        def cols(c0, width):
+            return slice(c0, c0 + width)
+
+        def entries(lst, c0, width):
+            return lst[:, c0 // 16 : (c0 + width) // 16]
+
+        l_offs, l_two, l1, l2, l3, l4, l5 = [sb("list%d" % i, [P, N // 16], U16) for i in range(7)]
+        xw = sb("xw", [P, T], U32)
+        xs = sb("xs", [P, T], U8)
+        w1raw = sb("w1raw", [P, 2 * N], U8)
+        w2raw = sb("w2raw", [P, 2 * N], U8)
+        w1sraw = sb("w1sraw", [P, N], U8)
+        w2sraw = sb("w2sraw", [P, N], U8)
+        tabs = planes("tab", N)
+        ga_sb = sb("ga_sb", [P, R], F32)
+        gb_sb = sb("gb_sb", [P, R], F32)
+
+        nc.gpsimd.memset(xs[:].bitcast(I32), 0)
+        nc.vector.memset(w1sraw[:].bitcast(I32), 0)
+        nc.vector.memset(w2sraw[:].bitcast(I32), 0)
+
+        tab_v = tab.rearrange("(p t) c -> p t c", t=R)
+
+        def load_scale_rows(queue, dst, src):
+            for r in range(4):
+                queue.dma_start(dst[r:P:32, :].bitcast(I32), src[0, r:16:4, :].bitcast(I32))
+
+        for e in range(2):
+            nc.gpsimd.dma_start(xs[e:P:16, :].bitcast(I32), x_scales[0, e:16:2, :].bitcast(I32))
+        nc.gpsimd.dma_start(ga_sb[:], ga.rearrange("(p t) o -> p (t o)", t=R))
+        nc.gpsimd.dma_start(gb_sb[:], gb.rearrange("(p t) o -> p (t o)", t=R))
+        nc.sync.dma_start(l_offs[:], offs)
+        nc.sync.dma_start(w1raw[:].bitcast(I32), w1_words[0].bitcast(I32))
+        nc.sync.dma_start(l2[:], n2)
+        nc.sync.dma_start(tabs[0][:], tab_v[:, 0, :])
+        nc.sync.dma_start(w2raw[:].bitcast(I32), w2_words[0].bitcast(I32))
+        nc.sync.dma_start(tabs[1][:], tab_v[:, 1, :])
+        nc.sync.dma_start(l_two[:], two)
+        nc.sync.dma_start(xw[:].bitcast(I32), x_words[0].rearrange("p n t -> p (n t)").bitcast(I32))
+        nc.sync.dma_start(tabs[2][:], tab_v[:, 2, :])
+        nc.sync.dma_start(tabs[3][:], tab_v[:, 3, :])
+        load_scale_rows(nc.sync, w1sraw, w1_scales)
+        nc.sync.dma_start(l1[:], n1)
+
+        sgn = sb("sgn", [P, R], F32)
+        sgn1 = sb("sgn1", [P, R], F32)
+        ga_abs = sb("ga_abs", [P, R], F32)
+        gb_sgn = sb("gb_sgn", [P, R], F32)
+        gb_half = sb("gb_half", [P, R], F32)
+        nc.gpsimd.tensor_scalar(sgn1[:], ga_sb[:], 0.0, 2.0, ALU.is_ge, ALU.mult)
+        nc.gpsimd.tensor_scalar(sgn[:], sgn1[:], 1.0, -1.0, ALU.mult, ALU.add)
+        nc.gpsimd.tensor_tensor(ga_abs[:], ga_sb[:], sgn[:], ALU.mult)
+        nc.gpsimd.tensor_tensor(gb_sgn[:], gb_sb[:], sgn[:], ALU.mult)
+        nc.gpsimd.tensor_scalar(gb_half[:], gb_sgn[:], -0.5, 0.0, ALU.mult, ALU.add)
+
+        def deal_words(name, raw):
+            words = sb(name, [P, 2 * N], U8)
+            nc.vector.tensor_copy(
+                words[:].rearrange("p (t m b) -> p t m b", t=R, b=2),
+                raw[:].rearrange("p (m t b) -> p t m b", t=R, b=2),
+            )
+            return words
+
+        def deal_scales(name, sraw):
+            scales = sb(name, [P, N], U8)
+            nc.vector.tensor_copy(
+                scales[:].rearrange("p (t m) -> p t m", t=R),
+                sraw[:].rearrange("p (m t) -> p t m", t=R),
+            )
+            return scales
+
+        w1w = deal_words("w1w", w1raw)
+        w2w = deal_words("w2w", w2raw)
+
+        picked_s = sb("picked_s", [P, N], U8)
+        xa_s = sb("xa_s", [P, N], U8)
+        xb_s = sb("xb_s", [P, N], U8)
+        nc.vector.tensor_copy(picked_s[:], xs[:].indirect(l_offs[:]))
+        nc.vector.tensor_copy(xa_s[:].bitcast(I32), picked_s[:].bitcast(I32))
+        for e in range(2):
+            nc.sync.dma_start(xa_s[2 + e : P : 32, :].bitcast(I32), picked_s[16 + e : P : 32, :].bitcast(I32))
+        for e in range(2):
+            nc.sync.dma_start(xs[2 + e : P : 32, :].bitcast(I32), x_scales[0, 2 + e : 16 : 4, :].bitcast(I32))
+        load_scale_rows(nc.sync, w2sraw, w2_scales)
+        nc.sync.dma_start(l3[:], n3)
+        nc.sync.dma_start(l4[:], n4)
+        nc.sync.dma_start(l5[:], n5)
+
+        def project(tag, words, scales, xq, xq_scales):
+            banks = []
+            for t in range(R):
+                bank = psum.tile([P, N], F32, name="%s%d" % (tag, t), tag="%s%d" % (tag, t))
+                nc.tensor.matmul_mx(
+                    out=bank[:],
+                    lhsT=words[:, cols(2 * P * t, 2 * P)].bitcast(FP4X4),
+                    lhsT_scale=scales[:, cols(P * t, P)],
+                    rhs=xq[:].bitcast(FP8X4),
+                    rhs_scale=xq_scales,
+                    start=True,
+                    stop=True,
+                )
+                banks.append(bank)
+            return banks
+
+        halves = [(0, HALF), (HALF, HALF)]
+
+        tabg = planes("tabg", N)
+        for t in range(R):
+            for c0, w in halves:
+                nc.scalar.activation(tabg[t][:, cols(c0, w)], tabs[t][:].indirect(entries(l2, c0, w)), ACT.Copy)
+
+        xa = sb("xa", [P, N], U32)
+        xb = sb("xb", [P, N], U32)
+        nc.vector.tensor_copy(xa[:], xw[:].indirect(l_offs[:]))
+        w1s = deal_scales("w1s", w1sraw)
+        a_ps = project("lo", w1w, w1s, xa, xa_s[:])
+        nc.vector.tensor_copy(xb[:], xw[:].indirect(l_two[:]))
+        nc.vector.tensor_copy(xb_s[:], xs[:].indirect(l_two[:]))
+        w2s = deal_scales("w2s", w2sraw)
+        b_ps = project("hi", w2w, w2s, xb, xb_s[:])
+
+        sg = planes("sg", N)
+        ap = planes("ap", N)
+        st = planes("st", N)
+        for t in range(R):
+            nc.scalar.activation(sg[t][:], a_ps[t][:], ACT.Sigmoid)
+            nc.scalar.activation(ap[t][:], a_ps[t][:], ACT.Copy, scale=ga_abs[:, t : t + 1])
+            for c0, w in halves:
+                nc.vector.tensor_tensor(
+                    st[t][:, cols(c0, w)], sg[t][:].indirect(entries(l1, c0, w)), ap[t][:, cols(c0, w)], ALU.mult
+                )
+
+        bw = planes("bw", N)
+        stg = planes("stg", N)
+        zf = sb("zf", [P, R, N], F32)
+        u = [sb("u%d" % h, [P, R, w], F32) for h, (c0, w) in enumerate(halves)]
+        bg = [sb("bg%d" % h, [P, R, w], F32) for h, (c0, w) in enumerate(halves)]
+        for t in range(R):
+            nc.scalar.activation(bw[t][:], b_ps[t][:], ACT.Copy, scale=gb_half[:, t : t + 1])
+            for c0, w in halves:
+                nc.scalar.activation(stg[t][:, cols(c0, w)], st[t][:].indirect(entries(l1, c0, w)), ACT.Copy)
+            for h, (c0, w) in enumerate(halves):
+                nc.vector.scalar_tensor_tensor(
+                    u[h][:, t, :], bw[t][:, cols(c0, w)], -2.0, tabg[t][:, cols(c0, w)], ALU.mult, ALU.mult
+                )
+            nc.vector.tensor_tensor(zf[:, t, :], st[t][:], stg[t][:], ALU.max)
+
+        for h, (c0, w) in enumerate(halves):
+            for t in range(R):
+                nc.scalar.activation(bg[h][:, t, :], bw[t][:].indirect(entries(l3, c0, w)), ACT.Copy)
+
+        zb = sb("zb", [P, R * N], BF16)
+        zq = sb("zq", [P, N], U32)
+        zs = sb("zs", [P, N], U8)
+        nc.vector.tensor_copy(
+            zb[:].rearrange("p (g e m k) -> p g m k e", g=2, e=2, k=R),
+            zf[:].rearrange("p k (m g e) -> p g m k e", g=2, e=2),
+        )
+        nc.vector.quantize_mx(out=zq[:].bitcast(FP8X4), scales=zs[:], in_=zb[:])
+
+        s = planes("s", N)
+        for h, (c0, w) in enumerate(halves):
+            z2b = sb("z2b%d" % h, [P, R * w], BF16)
+            z2q = sb("z2q%d" % h, [P, w], U32)
+            z2s = sb("z2s%d" % h, [P, w], U8)
+            nc.vector.tensor_tensor(
+                z2b[:].rearrange("p (c i k) -> p c k i", i=4, k=R),
+                bg[h][:].rearrange("p k (c i) -> p c k i", i=4),
+                u[h][:].rearrange("p k (c i) -> p c k i", i=4),
+                ALU.add,
+            )
+            nc.vector.quantize_mx(out=z2q[:].bitcast(FP8X4), scales=z2s[:], in_=z2b[:])
+            for t in range(R):
+                tag = "%s%d" % (("lo", "hi")[h], t)
+                bank = psum.tile([P, N], F32, name="s" + tag, tag=tag)
+                nc.tensor.matmul_mx(
+                    out=bank[:, 0:w],
+                    lhsT=zq[:, cols(P * t, P)].bitcast(FP8X4),
+                    lhsT_scale=zs[:, cols(P * t, P)],
+                    rhs=z2q[:].bitcast(FP8X4),
+                    rhs_scale=z2s[:],
+                    start=True,
+                    stop=True,
+                )
+                nc.scalar.activation(s[t][:, cols(c0, w)], bank[:, 0:w], ACT.Copy, scale=0.0625)
+
+        out_v = out_0.rearrange("(p t) v -> p t v", t=R)
+        words_v = out_1[0].rearrange("p n t -> p (n t)").bitcast(I32)
+        oq = sb("oq", [P, N], U32)
+        os_ = sb("os_", [P, N], U8)
+        pieces = [(0, 256), (256, 128), (384, 128)]
+        for h, (c0, w) in enumerate(pieces):
+            of = sb("of%d" % h, [P, R, w], F32)
+            ob = sb("ob%d" % h, [P, R * w], BF16)
+            for t in range(R):
+                g4 = sb("g4_%d_%d" % (h, t), [P, w], F32)
+                g5 = sb("g5_%d_%d" % (h, t), [P, w], F32)
+                m = sb("m_%d_%d" % (h, t), [P, w], F32)
+                nc.scalar.activation(g4[:], s[t][:].indirect(entries(l4, c0, w)), ACT.Copy)
+                if h == 0:
+                    nc.vector.tensor_copy(g5[:], s[t][:].indirect(entries(l5, c0, w)))
+                else:
+                    nc.scalar.activation(g5[:], s[t][:].indirect(entries(l5, c0, w)), ACT.Copy)
+                nc.vector.tensor_tensor(m[:], g4[:], g5[:], ALU.max)
+                nc.vector.scalar_tensor_tensor(of[:, t, :], s[t][:, cols(c0, w)], -0.75, m[:], ALU.mult, ALU.add)
+            nc.sync.dma_start(out_v[:, :, cols(c0, w)], of[:])
+            nc.vector.tensor_copy(
+                ob[:].rearrange("p (c i k) -> p c k i", i=4, k=R),
+                of[:].rearrange("p k (c i) -> p c k i", i=4),
+            )
+            nc.vector.quantize_mx(out=oq[:, cols(c0, w)].bitcast(FP8X4), scales=os_[:, cols(c0, w)], in_=ob[:])
+            nc.sync.dma_start(words_v[:, cols(c0, w)], oq[:, cols(c0, w)].bitcast(I32))
+        for q in range(4):
+            queue = (nc.sync, nc.scalar)[q % 2]
+            queue.dma_start(out_2[0, 4 * q : 4 * q + 4, :].bitcast(I32), os_[32 * q : 32 * q + 4, :].bitcast(I32))

@@ -30,8 +30,8 @@ def tile_picked_hkqtwicpkindgover_none_po_kernel(
         keep = ctx.enter_context(tc.tile_pool(name="keep", bufs=1))
         psum = ctx.enter_context(tc.psum_pool(name="psum", bufs=1))
 
-        def sb(name, shape, dtype):
-            return keep.tile(shape, dtype, name=name, align_bytes=64)
+        def sb(name, shape, dtype, tag=None):
+            return keep.tile(shape, dtype, name=name, tag=tag or name, align_bytes=64)
 
         def planes(name, width):
             return [sb("%s%d" % (name, t), [P, width], F32) for t in range(R)]
@@ -46,16 +46,13 @@ def tile_picked_hkqtwicpkindgover_none_po_kernel(
         xw = sb("xw", [P, T], U32)
         xs = sb("xs", [P, T], U8)
         w1raw = sb("w1raw", [P, 2 * N], U8)
-        w2raw = sb("w2raw", [P, 2 * N], U8)
         w1sraw = sb("w1sraw", [P, N], U8)
-        w2sraw = sb("w2sraw", [P, N], U8)
-        tabs = planes("tab", N)
-        ga_sb = sb("ga_sb", [P, R], F32)
-        gb_sb = sb("gb_sb", [P, R], F32)
+        tabs = planes("tab", 2 * N)
 
-        nc.gpsimd.memset(xs[:].bitcast(I32), 0)
+        nc.vector.memset(xs[:].bitcast(I32), 0)
         nc.vector.memset(w1sraw[:].bitcast(I32), 0)
-        nc.vector.memset(w2sraw[:].bitcast(I32), 0)
+        for t in range(R):
+            nc.vector.memset(tabs[t][:, N : 2 * N], 0.0)
 
         tab_v = tab.rearrange("(p t) c -> p t c", t=R)
 
@@ -63,33 +60,29 @@ def tile_picked_hkqtwicpkindgover_none_po_kernel(
             for r in range(4):
                 queue.dma_start(dst[r:P:32, :].bitcast(I32), src[0, r:16:4, :].bitcast(I32))
 
-        for e in range(2):
-            nc.gpsimd.dma_start(xs[e:P:16, :].bitcast(I32), x_scales[0, e:16:2, :].bitcast(I32))
-        nc.gpsimd.dma_start(ga_sb[:], ga.rearrange("(p t) o -> p (t o)", t=R))
-        nc.gpsimd.dma_start(gb_sb[:], gb.rearrange("(p t) o -> p (t o)", t=R))
         nc.sync.dma_start(l_offs[:], offs)
-        nc.sync.dma_start(w1raw[:].bitcast(I32), w1_words[0].bitcast(I32))
+        for e in range(2):
+            nc.sync.dma_start(xs[e:P:16, :].bitcast(I32), x_scales[0, e:16:2, :].bitcast(I32))
+        nc.gpsimd.dma_start(w1raw[:].bitcast(I32), w1_words[0].bitcast(I32))
+        load_scale_rows(nc.gpsimd, w1sraw, w1_scales)
         nc.sync.dma_start(l2[:], n2)
-        nc.sync.dma_start(tabs[0][:], tab_v[:, 0, :])
-        nc.sync.dma_start(w2raw[:].bitcast(I32), w2_words[0].bitcast(I32))
-        nc.sync.dma_start(tabs[1][:], tab_v[:, 1, :])
+        nc.sync.dma_start(tabs[0][:, 0:N], tab_v[:, 0, :])
         nc.sync.dma_start(l_two[:], two)
+        nc.sync.dma_start(tabs[1][:, 0:N], tab_v[:, 1, :])
         nc.sync.dma_start(xw[:].bitcast(I32), x_words[0].rearrange("p n t -> p (n t)").bitcast(I32))
-        nc.sync.dma_start(tabs[2][:], tab_v[:, 2, :])
-        nc.sync.dma_start(tabs[3][:], tab_v[:, 3, :])
-        load_scale_rows(nc.sync, w1sraw, w1_scales)
+        w2raw = sb("w2raw", [P, 2 * N], U8)
+        ga_sb = sb("ga_sb", [P, R], F32)
         nc.sync.dma_start(l1[:], n1)
+        nc.sync.dma_start(ga_sb[:], ga.rearrange("(p t) o -> p (t o)", t=R))
+        for t in range(2, R):
+            nc.sync.dma_start(tabs[t][:, 0:N], tab_v[:, t, :])
+        nc.sync.dma_start(w2raw[:].bitcast(I32), w2_words[0].bitcast(I32))
+        nc.sync.dma_start(l3[:], n3)
+        nc.sync.dma_start(l4[:], n4)
+        nc.sync.dma_start(l5[:], n5)
 
-        sgn = sb("sgn", [P, R], F32)
-        sgn1 = sb("sgn1", [P, R], F32)
-        ga_abs = sb("ga_abs", [P, R], F32)
-        gb_sgn = sb("gb_sgn", [P, R], F32)
-        gb_half = sb("gb_half", [P, R], F32)
-        nc.gpsimd.tensor_scalar(sgn1[:], ga_sb[:], 0.0, 2.0, ALU.is_ge, ALU.mult)
-        nc.gpsimd.tensor_scalar(sgn[:], sgn1[:], 1.0, -1.0, ALU.mult, ALU.add)
-        nc.gpsimd.tensor_tensor(ga_abs[:], ga_sb[:], sgn[:], ALU.mult)
-        nc.gpsimd.tensor_tensor(gb_sgn[:], gb_sb[:], sgn[:], ALU.mult)
-        nc.gpsimd.tensor_scalar(gb_half[:], gb_sgn[:], -0.5, 0.0, ALU.mult, ALU.add)
+        warm = sb("warm", [P, 8], F32)
+        nc.scalar.activation(warm[:, 0:1], tabs[0][:, N : N + 1], ACT.Sigmoid)
 
         def deal_words(name, raw):
             words = sb(name, [P, 2 * N], U8)
@@ -99,30 +92,23 @@ def tile_picked_hkqtwicpkindgover_none_po_kernel(
             )
             return words
 
-        def deal_scales(name, sraw):
+        def deal_scales(engine, name, sraw):
             scales = sb(name, [P, N], U8)
-            nc.vector.tensor_copy(
+            engine.tensor_copy(
                 scales[:].rearrange("p (t m) -> p t m", t=R),
                 sraw[:].rearrange("p (m t) -> p t m", t=R),
             )
             return scales
 
         w1w = deal_words("w1w", w1raw)
-        w2w = deal_words("w2w", w2raw)
 
-        picked_s = sb("picked_s", [P, N], U8)
-        xa_s = sb("xa_s", [P, N], U8)
-        xb_s = sb("xb_s", [P, N], U8)
-        nc.vector.tensor_copy(picked_s[:], xs[:].indirect(l_offs[:]))
-        nc.vector.tensor_copy(xa_s[:].bitcast(I32), picked_s[:].bitcast(I32))
+        picked_s = sb("picked_s", [P, 2 * N], U8)
+        xq_s = sb("xq_s", [P, 2 * N], U8)
+        nc.vector.tensor_copy(picked_s[:, 0:N], xs[:].indirect(l_offs[:]))
+        nc.vector.tensor_copy(picked_s[:, N : 2 * N], xs[:].indirect(l_two[:]))
+        nc.vector.tensor_copy(xq_s[:].bitcast(I32), picked_s[:].bitcast(I32))
         for e in range(2):
-            nc.sync.dma_start(xa_s[2 + e : P : 32, :].bitcast(I32), picked_s[16 + e : P : 32, :].bitcast(I32))
-        for e in range(2):
-            nc.sync.dma_start(xs[2 + e : P : 32, :].bitcast(I32), x_scales[0, 2 + e : 16 : 4, :].bitcast(I32))
-        load_scale_rows(nc.sync, w2sraw, w2_scales)
-        nc.sync.dma_start(l3[:], n3)
-        nc.sync.dma_start(l4[:], n4)
-        nc.sync.dma_start(l5[:], n5)
+            nc.sync.dma_start(xq_s[2 + e : P : 32, :].bitcast(I32), picked_s[16 + e : P : 32, :].bitcast(I32))
 
         def project(tag, words, scales, xq, xq_scales):
             banks = []
@@ -142,50 +128,57 @@ def tile_picked_hkqtwicpkindgover_none_po_kernel(
 
         halves = [(0, HALF), (HALF, HALF)]
 
-        tabg = planes("tabg", N)
+        sg = planes("sg", 2 * N)
+        st = planes("st", 2 * N)
+        tabg = [sg[t][:, N : 2 * N] for t in range(R)]
+        ap = [st[t][:, N : 2 * N] for t in range(R)]
         for t in range(R):
-            for c0, w in halves:
-                nc.scalar.activation(tabg[t][:, cols(c0, w)], tabs[t][:].indirect(entries(l2, c0, w)), ACT.Copy)
+            nc.scalar.activation(tabg[t], tabs[t][:].indirect(l2[:]), ACT.Copy)
+
+        w1s = deal_scales(nc.gpsimd, "w1s", w1sraw)
+        sgn = sb("sgn", [P, R], F32)
+        sgn1 = sb("sgn1", [P, R], F32)
+        ga_abs = sb("ga_abs", [P, R], F32)
+        gb_sgn = sb("gb_sgn", [P, R], F32)
+        gb_half = sb("gb_half", [P, R], F32)
+        nc.gpsimd.tensor_scalar(sgn1[:], ga_sb[:], 0.0, 2.0, ALU.is_ge, ALU.mult)
+        nc.gpsimd.tensor_scalar(sgn[:], sgn1[:], 1.0, -1.0, ALU.mult, ALU.add)
+        nc.gpsimd.tensor_tensor(ga_abs[:], ga_sb[:], sgn[:], ALU.mult)
+        gb_sb = sb("gb_sb", [P, R], F32, tag="tab2")
+        nc.sync.dma_start(gb_sb[:], gb.rearrange("(p t) o -> p (t o)", t=R))
+        nc.gpsimd.tensor_tensor(gb_sgn[:], gb_sb[:], sgn[:], ALU.mult)
+        nc.gpsimd.tensor_scalar(gb_half[:], gb_sgn[:], -0.5, 0.0, ALU.mult, ALU.add)
 
         xa = sb("xa", [P, N], U32)
         xb = sb("xb", [P, N], U32)
         nc.vector.tensor_copy(xa[:], xw[:].indirect(l_offs[:]))
-        w1s = deal_scales("w1s", w1sraw)
-        a_ps = project("lo", w1w, w1s, xa, xa_s[:])
+        load_scale_rows(nc.sync, w1sraw, w2_scales)
+        a_ps = project("lo", w1w, w1s, xa, xq_s[:, 0:N])
         nc.vector.tensor_copy(xb[:], xw[:].indirect(l_two[:]))
-        nc.vector.tensor_copy(xb_s[:], xs[:].indirect(l_two[:]))
-        w2s = deal_scales("w2s", w2sraw)
-        b_ps = project("hi", w2w, w2s, xb, xb_s[:])
+        w2w = deal_words("w2w", w2raw)
+        w2s = deal_scales(nc.gpsimd, "w2s", w1sraw)
+        b_ps = project("hi", w2w, w2s, xb, xq_s[:, N : 2 * N])
 
-        sg = planes("sg", N)
-        ap = planes("ap", N)
-        st = planes("st", N)
         for t in range(R):
-            nc.scalar.activation(sg[t][:], a_ps[t][:], ACT.Sigmoid)
-            nc.scalar.activation(ap[t][:], a_ps[t][:], ACT.Copy, scale=ga_abs[:, t : t + 1])
-            for c0, w in halves:
-                nc.vector.tensor_tensor(
-                    st[t][:, cols(c0, w)], sg[t][:].indirect(entries(l1, c0, w)), ap[t][:, cols(c0, w)], ALU.mult
-                )
+            nc.scalar.activation(sg[t][:, 0:N], a_ps[t][:], ACT.Sigmoid)
+            nc.scalar.activation(ap[t], a_ps[t][:], ACT.Copy, scale=ga_abs[:, t : t + 1])
+            nc.vector.tensor_tensor(st[t][:, 0:N], sg[t][:].indirect(l1[:]), ap[t], ALU.mult)
 
         bw = planes("bw", N)
         stg = planes("stg", N)
+        u = sb("u", [P, R, N], F32)
         zf = sb("zf", [P, R, N], F32)
-        u = [sb("u%d" % h, [P, R, w], F32) for h, (c0, w) in enumerate(halves)]
-        bg = [sb("bg%d" % h, [P, R, w], F32) for h, (c0, w) in enumerate(halves)]
+        z2lo = sb("z2lo", [P, R, HALF], F32)
+        bghi = sb("bghi", [P, R, HALF], F32)
         for t in range(R):
             nc.scalar.activation(bw[t][:], b_ps[t][:], ACT.Copy, scale=gb_half[:, t : t + 1])
-            for c0, w in halves:
-                nc.scalar.activation(stg[t][:, cols(c0, w)], st[t][:].indirect(entries(l1, c0, w)), ACT.Copy)
-            for h, (c0, w) in enumerate(halves):
-                nc.vector.scalar_tensor_tensor(
-                    u[h][:, t, :], bw[t][:, cols(c0, w)], -2.0, tabg[t][:, cols(c0, w)], ALU.mult, ALU.mult
-                )
-            nc.vector.tensor_tensor(zf[:, t, :], st[t][:], stg[t][:], ALU.max)
+            nc.scalar.activation(stg[t][:], st[t][:].indirect(l1[:]), ACT.Copy)
+            nc.vector.scalar_tensor_tensor(u[:, t, :], bw[t][:], -2.0, tabg[t], ALU.mult, ALU.mult)
+            nc.vector.tensor_tensor(z2lo[:, t, :], bw[t][:].indirect(entries(l3, 0, HALF)), u[:, t, 0:HALF], ALU.add)
+            nc.vector.tensor_tensor(zf[:, t, :], st[t][:, 0:N], stg[t][:], ALU.max)
 
-        for h, (c0, w) in enumerate(halves):
-            for t in range(R):
-                nc.scalar.activation(bg[h][:, t, :], bw[t][:].indirect(entries(l3, c0, w)), ACT.Copy)
+        for t in range(R):
+            nc.scalar.activation(bghi[:, t, :], bw[t][:].indirect(entries(l3, HALF, HALF)), ACT.Copy)
 
         zb = sb("zb", [P, R * N], BF16)
         zq = sb("zq", [P, N], U32)
@@ -197,16 +190,21 @@ def tile_picked_hkqtwicpkindgover_none_po_kernel(
         nc.vector.quantize_mx(out=zq[:].bitcast(FP8X4), scales=zs[:], in_=zb[:])
 
         s = planes("s", N)
+        last_banks = []
         for h, (c0, w) in enumerate(halves):
             z2b = sb("z2b%d" % h, [P, R * w], BF16)
             z2q = sb("z2q%d" % h, [P, w], U32)
             z2s = sb("z2s%d" % h, [P, w], U8)
-            nc.vector.tensor_tensor(
-                z2b[:].rearrange("p (c i k) -> p c k i", i=4, k=R),
-                bg[h][:].rearrange("p k (c i) -> p c k i", i=4),
-                u[h][:].rearrange("p k (c i) -> p c k i", i=4),
-                ALU.add,
-            )
+            z2b_v = z2b[:].rearrange("p (c i k) -> p c k i", i=4, k=R)
+            if h == 0:
+                nc.vector.tensor_copy(z2b_v, z2lo[:].rearrange("p k (c i) -> p c k i", i=4))
+            else:
+                nc.vector.tensor_tensor(
+                    z2b_v,
+                    bghi[:].rearrange("p k (c i) -> p c k i", i=4),
+                    u[:, :, HALF:N].rearrange("p k (c i) -> p c k i", i=4),
+                    ALU.add,
+                )
             nc.vector.quantize_mx(out=z2q[:].bitcast(FP8X4), scales=z2s[:], in_=z2b[:])
             for t in range(R):
                 tag = "%s%d" % (("lo", "hi")[h], t)
@@ -220,7 +218,10 @@ def tile_picked_hkqtwicpkindgover_none_po_kernel(
                     start=True,
                     stop=True,
                 )
-                nc.scalar.activation(s[t][:, cols(c0, w)], bank[:, 0:w], ACT.Copy, scale=0.0625)
+                if h == 0:
+                    nc.scalar.activation(s[t][:, cols(c0, w)], bank[:, 0:w], ACT.Copy, scale=0.0625)
+                else:
+                    last_banks.append(bank)
 
         out_v = out_0.rearrange("(p t) v -> p t v", t=R)
         words_v = out_1[0].rearrange("p n t -> p (n t)").bitcast(I32)
@@ -234,8 +235,10 @@ def tile_picked_hkqtwicpkindgover_none_po_kernel(
                 g4 = sb("g4_%d_%d" % (h, t), [P, w], F32)
                 g5 = sb("g5_%d_%d" % (h, t), [P, w], F32)
                 m = sb("m_%d_%d" % (h, t), [P, w], F32)
-                nc.scalar.activation(g4[:], s[t][:].indirect(entries(l4, c0, w)), ACT.Copy)
                 if h == 0:
+                    nc.scalar.activation(s[t][:, HALF:N], last_banks[t][:, 0:HALF], ACT.Copy, scale=0.0625)
+                nc.scalar.activation(g4[:], s[t][:].indirect(entries(l4, c0, w)), ACT.Copy)
+                if h == 0 or (h == 1 and t < 2):
                     nc.vector.tensor_copy(g5[:], s[t][:].indirect(entries(l5, c0, w)))
                 else:
                     nc.scalar.activation(g5[:], s[t][:].indirect(entries(l5, c0, w)), ACT.Copy)

@@ -63,20 +63,20 @@ def tile_picked_hkqtwicpkindgover_none_po_kernel(
         nc.sync.dma_start(l_offs[:], offs)
         for e in range(2):
             nc.sync.dma_start(xs[e:P:16, :].bitcast(I32), x_scales[0, e:16:2, :].bitcast(I32))
-        nc.gpsimd.dma_start(w1raw[:].bitcast(I32), w1_words[0].bitcast(I32))
-        load_scale_rows(nc.gpsimd, w1sraw, w1_scales)
         nc.sync.dma_start(l2[:], n2)
         nc.sync.dma_start(tabs[0][:, 0:N], tab_v[:, 0, :])
+        nc.sync.dma_start(w1raw[:].bitcast(I32), w1_words[0].bitcast(I32))
         nc.sync.dma_start(l_two[:], two)
-        nc.sync.dma_start(tabs[1][:, 0:N], tab_v[:, 1, :])
         nc.sync.dma_start(xw[:].bitcast(I32), x_words[0].rearrange("p n t -> p (n t)").bitcast(I32))
-        w2raw = sb("w2raw", [P, 2 * N], U8)
+        load_scale_rows(nc.sync, w1sraw, w1_scales)
         ga_sb = sb("ga_sb", [P, R], F32)
         nc.sync.dma_start(l1[:], n1)
-        nc.sync.dma_start(ga_sb[:], ga.rearrange("(p t) o -> p (t o)", t=R))
-        for t in range(2, R):
-            nc.sync.dma_start(tabs[t][:, 0:N], tab_v[:, t, :])
+        nc.sync.dma_start(tabs[1][:, 0:N], tab_v[:, 1, :])
+        nc.sync.dma_start(tabs[2][:, 0:N], tab_v[:, 2, :])
+        w2raw = sb("w2raw", [P, 2 * N], U8)
         nc.sync.dma_start(w2raw[:].bitcast(I32), w2_words[0].bitcast(I32))
+        nc.sync.dma_start(tabs[3][:, 0:N], tab_v[:, 3, :])
+        nc.sync.dma_start(ga_sb[:], ga.rearrange("(p t) o -> p (t o)", t=R))
         nc.sync.dma_start(l3[:], n3)
         nc.sync.dma_start(l4[:], n4)
         nc.sync.dma_start(l5[:], n5)
@@ -92,9 +92,9 @@ def tile_picked_hkqtwicpkindgover_none_po_kernel(
             )
             return words
 
-        def deal_scales(engine, name, sraw):
-            scales = sb(name, [P, N], U8)
-            engine.tensor_copy(
+        def deal_scales(name, sraw, tag=None):
+            scales = sb(name, [P, N], U8, tag=tag)
+            nc.vector.tensor_copy(
                 scales[:].rearrange("p (t m) -> p t m", t=R),
                 sraw[:].rearrange("p (m t) -> p t m", t=R),
             )
@@ -135,29 +135,25 @@ def tile_picked_hkqtwicpkindgover_none_po_kernel(
         for t in range(R):
             nc.scalar.activation(tabg[t], tabs[t][:].indirect(l2[:]), ACT.Copy)
 
-        w1s = deal_scales(nc.gpsimd, "w1s", w1sraw)
-        sgn = sb("sgn", [P, R], F32)
-        sgn1 = sb("sgn1", [P, R], F32)
-        ga_abs = sb("ga_abs", [P, R], F32)
-        gb_sgn = sb("gb_sgn", [P, R], F32)
-        gb_half = sb("gb_half", [P, R], F32)
-        nc.gpsimd.tensor_scalar(sgn1[:], ga_sb[:], 0.0, 2.0, ALU.is_ge, ALU.mult)
-        nc.gpsimd.tensor_scalar(sgn[:], sgn1[:], 1.0, -1.0, ALU.mult, ALU.add)
-        nc.gpsimd.tensor_tensor(ga_abs[:], ga_sb[:], sgn[:], ALU.mult)
-        gb_sb = sb("gb_sb", [P, R], F32, tag="tab2")
-        nc.sync.dma_start(gb_sb[:], gb.rearrange("(p t) o -> p (t o)", t=R))
-        nc.gpsimd.tensor_tensor(gb_sgn[:], gb_sb[:], sgn[:], ALU.mult)
-        nc.gpsimd.tensor_scalar(gb_half[:], gb_sgn[:], -0.5, 0.0, ALU.mult, ALU.add)
-
         xa = sb("xa", [P, N], U32)
         xb = sb("xb", [P, N], U32)
         nc.vector.tensor_copy(xa[:], xw[:].indirect(l_offs[:]))
+        w1s = deal_scales("w1s", w1sraw)
         load_scale_rows(nc.sync, w1sraw, w2_scales)
         a_ps = project("lo", w1w, w1s, xa, xq_s[:, 0:N])
         nc.vector.tensor_copy(xb[:], xw[:].indirect(l_two[:]))
+        gb_sb = sb("gb_sb", [P, R], F32, tag="tab1")
+        nc.sync.dma_start(gb_sb[:], gb.rearrange("(p t) o -> p (t o)", t=R))
         w2w = deal_words("w2w", w2raw)
-        w2s = deal_scales(nc.gpsimd, "w2s", w1sraw)
+        w2s = deal_scales("w2s", w1sraw, tag="xa")
         b_ps = project("hi", w2w, w2s, xb, xq_s[:, N : 2 * N])
+
+        half_sign = sb("half_sign", [P, R], F32)
+        ga_abs = sb("ga_abs", [P, R], F32)
+        gb_half = sb("gb_half", [P, R], F32, tag="w1s")
+        nc.vector.tensor_scalar(half_sign[:], ga_sb[:], 0.0, -0.5, ALU.is_ge, ALU.add)
+        nc.vector.scalar_tensor_tensor(ga_abs[:], ga_sb[:], 2.0, half_sign[:], ALU.mult, ALU.mult)
+        nc.vector.scalar_tensor_tensor(gb_half[:], gb_sb[:], -1.0, half_sign[:], ALU.mult, ALU.mult)
 
         for t in range(R):
             nc.scalar.activation(sg[t][:, 0:N], a_ps[t][:], ACT.Sigmoid)
@@ -169,7 +165,7 @@ def tile_picked_hkqtwicpkindgover_none_po_kernel(
         u = sb("u", [P, R, N], F32)
         zf = sb("zf", [P, R, N], F32)
         z2lo = sb("z2lo", [P, R, HALF], F32)
-        bghi = sb("bghi", [P, R, HALF], F32)
+        z2hi = sb("z2hi", [P, R, HALF], F32)
         for t in range(R):
             nc.scalar.activation(bw[t][:], b_ps[t][:], ACT.Copy, scale=gb_half[:, t : t + 1])
             nc.scalar.activation(stg[t][:], st[t][:].indirect(l1[:]), ACT.Copy)
@@ -177,80 +173,103 @@ def tile_picked_hkqtwicpkindgover_none_po_kernel(
             nc.vector.tensor_tensor(z2lo[:, t, :], bw[t][:].indirect(entries(l3, 0, HALF)), u[:, t, 0:HALF], ALU.add)
             nc.vector.tensor_tensor(zf[:, t, :], st[t][:, 0:N], stg[t][:], ALU.max)
 
+        bg = sb("bg", [P, R, HALF], F32)
         for t in range(R):
-            nc.scalar.activation(bghi[:, t, :], bw[t][:].indirect(entries(l3, HALF, HALF)), ACT.Copy)
+            nc.scalar.activation(bg[:, t, :], bw[t][:].indirect(entries(l3, HALF, HALF)), ACT.Copy)
 
         zb = sb("zb", [P, R * N], BF16)
         zq = sb("zq", [P, N], U32)
         zs = sb("zs", [P, N], U8)
+        z2b = [sb("z2b%d" % h, [P, R * HALF], BF16) for h in range(2)]
+        z2q = [sb("z2q%d" % h, [P, HALF], U32) for h in range(2)]
+        z2s = [sb("z2s%d" % h, [P, HALF], U8) for h in range(2)]
+
+        def interleave(dst, src):
+            nc.vector.tensor_copy(
+                dst[:].rearrange("p (c i k) -> p c k i", i=4, k=R),
+                src[:].rearrange("p k (c i) -> p c k i", i=4),
+            )
+
+        def quantize_z(g):
+            nc.vector.quantize_mx(
+                out=zq[:, cols(g * HALF, HALF)].bitcast(FP8X4),
+                scales=zs[:, cols(g * HALF, HALF)],
+                in_=zb[:, cols(g * R * HALF, R * HALF)],
+            )
+
+        def quantize_z2(h):
+            nc.vector.quantize_mx(out=z2q[h][:].bitcast(FP8X4), scales=z2s[h][:], in_=z2b[h][:])
+
+        s = planes("s", N)
+
+        def product(h, t):
+            tag = "%s%d" % (("lo", "hi")[h], t)
+            bank = psum.tile([P, N], F32, name="s" + tag, tag=tag)
+            nc.tensor.matmul_mx(
+                out=bank[:, 0:HALF],
+                lhsT=zq[:, cols(P * t, P)].bitcast(FP8X4),
+                lhsT_scale=zs[:, cols(P * t, P)],
+                rhs=z2q[h][:].bitcast(FP8X4),
+                rhs_scale=z2s[h][:],
+                start=True,
+                stop=True,
+            )
+            nc.scalar.activation(s[t][:, cols(h * HALF, HALF)], bank[:, 0:HALF], ACT.Copy, scale=0.0625)
+
+        interleave(z2b[0], z2lo)
         nc.vector.tensor_copy(
             zb[:].rearrange("p (g e m k) -> p g m k e", g=2, e=2, k=R),
             zf[:].rearrange("p k (m g e) -> p g m k e", g=2, e=2),
         )
-        nc.vector.quantize_mx(out=zq[:].bitcast(FP8X4), scales=zs[:], in_=zb[:])
-
-        s = planes("s", N)
-        last_banks = []
-        for h, (c0, w) in enumerate(halves):
-            z2b = sb("z2b%d" % h, [P, R * w], BF16)
-            z2q = sb("z2q%d" % h, [P, w], U32)
-            z2s = sb("z2s%d" % h, [P, w], U8)
-            z2b_v = z2b[:].rearrange("p (c i k) -> p c k i", i=4, k=R)
-            if h == 0:
-                nc.vector.tensor_copy(z2b_v, z2lo[:].rearrange("p k (c i) -> p c k i", i=4))
-            else:
-                nc.vector.tensor_tensor(
-                    z2b_v,
-                    bghi[:].rearrange("p k (c i) -> p c k i", i=4),
-                    u[:, :, HALF:N].rearrange("p k (c i) -> p c k i", i=4),
-                    ALU.add,
-                )
-            nc.vector.quantize_mx(out=z2q[:].bitcast(FP8X4), scales=z2s[:], in_=z2b[:])
-            for t in range(R):
-                tag = "%s%d" % (("lo", "hi")[h], t)
-                bank = psum.tile([P, N], F32, name="s" + tag, tag=tag)
-                nc.tensor.matmul_mx(
-                    out=bank[:, 0:w],
-                    lhsT=zq[:, cols(P * t, P)].bitcast(FP8X4),
-                    lhsT_scale=zs[:, cols(P * t, P)],
-                    rhs=z2q[:].bitcast(FP8X4),
-                    rhs_scale=z2s[:],
-                    start=True,
-                    stop=True,
-                )
-                if h == 0:
-                    nc.scalar.activation(s[t][:, cols(c0, w)], bank[:, 0:w], ACT.Copy, scale=0.0625)
-                else:
-                    last_banks.append(bank)
+        quantize_z2(0)
+        quantize_z(0)
+        product(0, 0)
+        product(0, 1)
+        nc.vector.tensor_tensor(z2hi[:], bg[:], u[:, :, HALF:N], ALU.add)
+        quantize_z(1)
+        product(0, 2)
+        product(0, 3)
+        interleave(z2b[1], z2hi)
+        quantize_z2(1)
+        for t in range(R):
+            product(1, t)
 
         out_v = out_0.rearrange("(p t) v -> p t v", t=R)
         words_v = out_1[0].rearrange("p n t -> p (n t)").bitcast(I32)
         oq = sb("oq", [P, N], U32)
         os_ = sb("os_", [P, N], U8)
         pieces = [(0, 256), (256, 128), (384, 128)]
-        for h, (c0, w) in enumerate(pieces):
-            of = sb("of%d" % h, [P, R, w], F32)
-            ob = sb("ob%d" % h, [P, R * w], BF16)
-            for t in range(R):
-                g4 = sb("g4_%d_%d" % (h, t), [P, w], F32)
-                g5 = sb("g5_%d_%d" % (h, t), [P, w], F32)
-                m = sb("m_%d_%d" % (h, t), [P, w], F32)
-                if h == 0:
-                    nc.scalar.activation(s[t][:, HALF:N], last_banks[t][:, 0:HALF], ACT.Copy, scale=0.0625)
-                nc.scalar.activation(g4[:], s[t][:].indirect(entries(l4, c0, w)), ACT.Copy)
-                if h == 0 or (h == 1 and t < 2):
-                    nc.vector.tensor_copy(g5[:], s[t][:].indirect(entries(l5, c0, w)))
-                else:
-                    nc.scalar.activation(g5[:], s[t][:].indirect(entries(l5, c0, w)), ACT.Copy)
-                nc.vector.tensor_tensor(m[:], g4[:], g5[:], ALU.max)
-                nc.vector.scalar_tensor_tensor(of[:, t, :], s[t][:, cols(c0, w)], -0.75, m[:], ALU.mult, ALU.add)
-            nc.sync.dma_start(out_v[:, :, cols(c0, w)], of[:])
-            nc.vector.tensor_copy(
-                ob[:].rearrange("p (c i k) -> p c k i", i=4, k=R),
-                of[:].rearrange("p k (c i) -> p c k i", i=4),
-            )
+
+        obs = [sb("ob%d" % h, [P, R * w], BF16) for h, (c0, w) in enumerate(pieces)]
+
+        def hand_on(h):
+            c0, w = pieces[h]
+            ob = obs[h]
             nc.vector.quantize_mx(out=oq[:, cols(c0, w)].bitcast(FP8X4), scales=os_[:, cols(c0, w)], in_=ob[:])
             nc.sync.dma_start(words_v[:, cols(c0, w)], oq[:, cols(c0, w)].bitcast(I32))
+
+        for h, (c0, w) in enumerate(pieces):
+            of = sb("of%d" % h, [P, R, w], F32)
+            g4 = sb("g4_%d" % h, [P, R, w], F32)
+            g5 = sb("g5_%d" % h, [P, R, w], F32)
+            m = sb("m_%d" % h, [P, R, w], F32)
+            for t in range(R):
+                nc.scalar.activation(g4[:, t, :], s[t][:].indirect(entries(l4, c0, w)), ACT.Copy)
+                if h == 0:
+                    nc.vector.tensor_copy(g5[:, t, :], s[t][:].indirect(entries(l5, c0, w)))
+                else:
+                    nc.scalar.activation(g5[:, t, :], s[t][:].indirect(entries(l5, c0, w)), ACT.Copy)
+            nc.vector.tensor_tensor(m[:, 0:2, :], g4[:, 0:2, :], g5[:, 0:2, :], ALU.max)
+            if h > 0:
+                hand_on(h - 1)
+            nc.vector.tensor_tensor(m[:, 2:4, :], g4[:, 2:4, :], g5[:, 2:4, :], ALU.max)
+            for t in range(R):
+                nc.vector.scalar_tensor_tensor(
+                    of[:, t, :], s[t][:, cols(c0, w)], -0.75, m[:, t, :], ALU.mult, ALU.add
+                )
+            nc.sync.dma_start(out_v[:, :, cols(c0, w)], of[:])
+            interleave(obs[h], of)
+        hand_on(len(pieces) - 1)
         for q in range(4):
             queue = (nc.sync, nc.scalar)[q % 2]
             queue.dma_start(out_2[0, 4 * q : 4 * q + 4, :].bitcast(I32), os_[32 * q : 32 * q + 4, :].bitcast(I32))

@@ -17,8 +17,12 @@ P = 128
 R = 4
 N = 512
 T = 2048
-HALF = 256
-FLOPS = 3 * 2 * 512 * 512 * 512
+GROUP = 16
+QUAD = 32
+HALF = N // 2
+PIECES = ((0, 256), (256, 128), (384, 128))
+N5_PLANES_ON_VECTOR = (4, 2, 0)
+FLOPS = 3 * 2 * N * N * N
 
 
 def tile_picked_hkqtwicpkindgover_none_po_kernel(
@@ -36,39 +40,39 @@ def tile_picked_hkqtwicpkindgover_none_po_kernel(
         def planes(name, width):
             return [sb("%s%d" % (name, t), [P, width], F32) for t in range(R)]
 
-        def cols(c0, width):
-            return slice(c0, c0 + width)
+        def cols(first, width):
+            return slice(first, first + width)
 
-        def entries(lst, c0, width):
-            return lst[:, c0 // 16 : (c0 + width) // 16]
+        def entries(list_tile, first, width):
+            return list_tile[:, first // GROUP : (first + width) // GROUP]
 
-        l_offs, l_two, l1, l2, l3, l4, l5 = [sb("list%d" % i, [P, N // 16], U16) for i in range(7)]
+        l_offs, l_two, l1, l2, l3, l4, l5 = [sb("list%d" % i, [P, N // GROUP], U16) for i in range(7)]
         xw = sb("xw", [P, T], U32)
         xs = sb("xs", [P, T], U8)
         w1raw = sb("w1raw", [P, 2 * N], U8)
-        w1sraw = sb("w1sraw", [P, N], U8)
+        ws_stage = sb("ws_stage", [P, N], U8)
         tabs = planes("tab", 2 * N)
 
         nc.vector.memset(xs[:].bitcast(I32), 0)
-        nc.vector.memset(w1sraw[:].bitcast(I32), 0)
+        nc.vector.memset(ws_stage[:].bitcast(I32), 0)
         for t in range(R):
             nc.vector.memset(tabs[t][:, N : 2 * N], 0.0)
 
         tab_v = tab.rearrange("(p t) c -> p t c", t=R)
 
-        def load_scale_rows(queue, dst, src):
+        def load_weight_scales(src):
             for r in range(4):
-                queue.dma_start(dst[r:P:32, :].bitcast(I32), src[0, r:16:4, :].bitcast(I32))
+                nc.sync.dma_start(ws_stage[r:P:QUAD, :].bitcast(I32), src[0, r:16:4, :].bitcast(I32))
 
         nc.sync.dma_start(l_offs[:], offs)
         for e in range(2):
-            nc.sync.dma_start(xs[e:P:16, :].bitcast(I32), x_scales[0, e:16:2, :].bitcast(I32))
+            nc.sync.dma_start(xs[e:P:GROUP, :].bitcast(I32), x_scales[0, e:16:2, :].bitcast(I32))
         nc.sync.dma_start(l2[:], n2)
         nc.sync.dma_start(tabs[0][:, 0:N], tab_v[:, 0, :])
         nc.sync.dma_start(w1raw[:].bitcast(I32), w1_words[0].bitcast(I32))
         nc.sync.dma_start(l_two[:], two)
         nc.sync.dma_start(xw[:].bitcast(I32), x_words[0].rearrange("p n t -> p (n t)").bitcast(I32))
-        load_scale_rows(nc.sync, w1sraw, w1_scales)
+        load_weight_scales(w1_scales)
         ga_sb = sb("ga_sb", [P, R], F32)
         nc.sync.dma_start(l1[:], n1)
         nc.sync.dma_start(tabs[1][:, 0:N], tab_v[:, 1, :])
@@ -92,11 +96,11 @@ def tile_picked_hkqtwicpkindgover_none_po_kernel(
             )
             return words
 
-        def deal_scales(name, sraw, tag=None):
+        def deal_scales(name, tag=None):
             scales = sb(name, [P, N], U8, tag=tag)
             nc.vector.tensor_copy(
                 scales[:].rearrange("p (t m) -> p t m", t=R),
-                sraw[:].rearrange("p (m t) -> p t m", t=R),
+                ws_stage[:].rearrange("p (m t) -> p t m", t=R),
             )
             return scales
 
@@ -108,44 +112,44 @@ def tile_picked_hkqtwicpkindgover_none_po_kernel(
         nc.vector.tensor_copy(picked_s[:, N : 2 * N], xs[:].indirect(l_two[:]))
         nc.vector.tensor_copy(xq_s[:].bitcast(I32), picked_s[:].bitcast(I32))
         for e in range(2):
-            nc.sync.dma_start(xq_s[2 + e : P : 32, :].bitcast(I32), picked_s[16 + e : P : 32, :].bitcast(I32))
+            nc.sync.dma_start(
+                xq_s[2 + e : P : QUAD, :].bitcast(I32), picked_s[GROUP + e : P : QUAD, :].bitcast(I32)
+            )
 
-        def project(tag, words, scales, xq, xq_scales):
+        def project(banks_tag, words, scales, picked_words, picked_scales):
             banks = []
             for t in range(R):
-                bank = psum.tile([P, N], F32, name="%s%d" % (tag, t), tag="%s%d" % (tag, t))
+                bank = psum.tile([P, N], F32, name="%s%d" % (banks_tag, t), tag="%s%d" % (banks_tag, t))
                 nc.tensor.matmul_mx(
                     out=bank[:],
                     lhsT=words[:, cols(2 * P * t, 2 * P)].bitcast(FP4X4),
                     lhsT_scale=scales[:, cols(P * t, P)],
-                    rhs=xq[:].bitcast(FP8X4),
-                    rhs_scale=xq_scales,
+                    rhs=picked_words[:].bitcast(FP8X4),
+                    rhs_scale=picked_scales,
                     start=True,
                     stop=True,
                 )
                 banks.append(bank)
             return banks
 
-        halves = [(0, HALF), (HALF, HALF)]
-
         sg = planes("sg", 2 * N)
         st = planes("st", 2 * N)
-        tabg = [sg[t][:, N : 2 * N] for t in range(R)]
-        ap = [st[t][:, N : 2 * N] for t in range(R)]
+        tab_n2 = [sg[t][:, N : 2 * N] for t in range(R)]
+        a_scaled = [st[t][:, N : 2 * N] for t in range(R)]
         for t in range(R):
-            nc.scalar.activation(tabg[t], tabs[t][:].indirect(l2[:]), ACT.Copy)
+            nc.scalar.activation(tab_n2[t], tabs[t][:].indirect(l2[:]), ACT.Copy)
 
         xa = sb("xa", [P, N], U32)
         xb = sb("xb", [P, N], U32)
         nc.vector.tensor_copy(xa[:], xw[:].indirect(l_offs[:]))
-        w1s = deal_scales("w1s", w1sraw)
-        load_scale_rows(nc.sync, w1sraw, w2_scales)
+        w1s = deal_scales("w1s")
+        load_weight_scales(w2_scales)
         a_ps = project("lo", w1w, w1s, xa, xq_s[:, 0:N])
         nc.vector.tensor_copy(xb[:], xw[:].indirect(l_two[:]))
         gb_sb = sb("gb_sb", [P, R], F32, tag="tab1")
         nc.sync.dma_start(gb_sb[:], gb.rearrange("(p t) o -> p (t o)", t=R))
         w2w = deal_words("w2w", w2raw)
-        w2s = deal_scales("w2s", w1sraw, tag="xa")
+        w2s = deal_scales("w2s", tag="xa")
         b_ps = project("hi", w2w, w2s, xb, xq_s[:, N : 2 * N])
 
         half_sign = sb("half_sign", [P, R], F32)
@@ -157,32 +161,33 @@ def tile_picked_hkqtwicpkindgover_none_po_kernel(
 
         for t in range(R):
             nc.scalar.activation(sg[t][:, 0:N], a_ps[t][:], ACT.Sigmoid)
-            nc.scalar.activation(ap[t], a_ps[t][:], ACT.Copy, scale=ga_abs[:, t : t + 1])
-            nc.vector.tensor_tensor(st[t][:, 0:N], sg[t][:].indirect(l1[:]), ap[t], ALU.mult)
+            nc.scalar.activation(a_scaled[t], a_ps[t][:], ACT.Copy, scale=ga_abs[:, t : t + 1])
+            nc.vector.tensor_tensor(st[t][:, 0:N], sg[t][:].indirect(l1[:]), a_scaled[t], ALU.mult)
 
-        bw = planes("bw", N)
-        stg = planes("stg", N)
-        u = sb("u", [P, R, N], F32)
-        zf = sb("zf", [P, R, N], F32)
-        z2lo = sb("z2lo", [P, R, HALF], F32)
-        z2hi = sb("z2hi", [P, R, HALF], F32)
+        b_half = planes("b_half", N)
+        st_n1 = planes("st_n1", N)
+        b_tab = sb("b_tab", [P, R, N], F32)
+        z = sb("z", [P, R, N], F32)
+        z2 = [sb("z2_%d" % h, [P, R, HALF], F32) for h in range(2)]
         for t in range(R):
-            nc.scalar.activation(bw[t][:], b_ps[t][:], ACT.Copy, scale=gb_half[:, t : t + 1])
-            nc.scalar.activation(stg[t][:], st[t][:].indirect(l1[:]), ACT.Copy)
-            nc.vector.scalar_tensor_tensor(u[:, t, :], bw[t][:], -2.0, tabg[t], ALU.mult, ALU.mult)
-            nc.vector.tensor_tensor(z2lo[:, t, :], bw[t][:].indirect(entries(l3, 0, HALF)), u[:, t, 0:HALF], ALU.add)
-            nc.vector.tensor_tensor(zf[:, t, :], st[t][:, 0:N], stg[t][:], ALU.max)
+            nc.scalar.activation(b_half[t][:], b_ps[t][:], ACT.Copy, scale=gb_half[:, t : t + 1])
+            nc.scalar.activation(st_n1[t][:], st[t][:].indirect(l1[:]), ACT.Copy)
+            nc.vector.scalar_tensor_tensor(b_tab[:, t, :], b_half[t][:], -2.0, tab_n2[t], ALU.mult, ALU.mult)
+            nc.vector.tensor_tensor(
+                z2[0][:, t, :], b_half[t][:].indirect(entries(l3, 0, HALF)), b_tab[:, t, 0:HALF], ALU.add
+            )
+            nc.vector.tensor_tensor(z[:, t, :], st[t][:, 0:N], st_n1[t][:], ALU.max)
 
-        bg = sb("bg", [P, R, HALF], F32)
+        b_n3 = sb("b_n3", [P, R, HALF], F32)
         for t in range(R):
-            nc.scalar.activation(bg[:, t, :], bw[t][:].indirect(entries(l3, HALF, HALF)), ACT.Copy)
+            nc.scalar.activation(b_n3[:, t, :], b_half[t][:].indirect(entries(l3, HALF, HALF)), ACT.Copy)
 
-        zb = sb("zb", [P, R * N], BF16)
-        zq = sb("zq", [P, N], U32)
-        zs = sb("zs", [P, N], U8)
-        z2b = [sb("z2b%d" % h, [P, R * HALF], BF16) for h in range(2)]
-        z2q = [sb("z2q%d" % h, [P, HALF], U32) for h in range(2)]
-        z2s = [sb("z2s%d" % h, [P, HALF], U8) for h in range(2)]
+        z_bf = sb("z_bf", [P, R * N], BF16)
+        z_words = sb("z_words", [P, N], U32)
+        z_scales = sb("z_scales", [P, N], U8)
+        z2_bf = [sb("z2_bf%d" % h, [P, R * HALF], BF16) for h in range(2)]
+        z2_words = [sb("z2_words%d" % h, [P, HALF], U32) for h in range(2)]
+        z2_scales = [sb("z2_scales%d" % h, [P, HALF], U8) for h in range(2)]
 
         def interleave(dst, src):
             nc.vector.tensor_copy(
@@ -192,84 +197,88 @@ def tile_picked_hkqtwicpkindgover_none_po_kernel(
 
         def quantize_z(g):
             nc.vector.quantize_mx(
-                out=zq[:, cols(g * HALF, HALF)].bitcast(FP8X4),
-                scales=zs[:, cols(g * HALF, HALF)],
-                in_=zb[:, cols(g * R * HALF, R * HALF)],
+                out=z_words[:, cols(2 * P * g, 2 * P)].bitcast(FP8X4),
+                scales=z_scales[:, cols(2 * P * g, 2 * P)],
+                in_=z_bf[:, cols(2 * P * R * g, 2 * P * R)],
             )
 
         def quantize_z2(h):
-            nc.vector.quantize_mx(out=z2q[h][:].bitcast(FP8X4), scales=z2s[h][:], in_=z2b[h][:])
+            nc.vector.quantize_mx(out=z2_words[h][:].bitcast(FP8X4), scales=z2_scales[h][:], in_=z2_bf[h][:])
 
         s = planes("s", N)
 
         def product(h, t):
-            tag = "%s%d" % (("lo", "hi")[h], t)
-            bank = psum.tile([P, N], F32, name="s" + tag, tag=tag)
+            banks_tag = "%s%d" % (("lo", "hi")[h], t)
+            bank = psum.tile([P, N], F32, name="s" + banks_tag, tag=banks_tag)
             nc.tensor.matmul_mx(
                 out=bank[:, 0:HALF],
-                lhsT=zq[:, cols(P * t, P)].bitcast(FP8X4),
-                lhsT_scale=zs[:, cols(P * t, P)],
-                rhs=z2q[h][:].bitcast(FP8X4),
-                rhs_scale=z2s[h][:],
+                lhsT=z_words[:, cols(P * t, P)].bitcast(FP8X4),
+                lhsT_scale=z_scales[:, cols(P * t, P)],
+                rhs=z2_words[h][:].bitcast(FP8X4),
+                rhs_scale=z2_scales[h][:],
                 start=True,
                 stop=True,
             )
             nc.scalar.activation(s[t][:, cols(h * HALF, HALF)], bank[:, 0:HALF], ACT.Copy, scale=0.0625)
 
-        interleave(z2b[0], z2lo)
+        interleave(z2_bf[0], z2[0])
         nc.vector.tensor_copy(
-            zb[:].rearrange("p (g e m k) -> p g m k e", g=2, e=2, k=R),
-            zf[:].rearrange("p k (m g e) -> p g m k e", g=2, e=2),
+            z_bf[:].rearrange("p (g e m k) -> p g m k e", g=2, e=2, k=R),
+            z[:].rearrange("p k (m g e) -> p g m k e", g=2, e=2),
         )
         quantize_z2(0)
         quantize_z(0)
         product(0, 0)
         product(0, 1)
-        nc.vector.tensor_tensor(z2hi[:], bg[:], u[:, :, HALF:N], ALU.add)
+        nc.vector.tensor_tensor(z2[1][:], b_n3[:], b_tab[:, :, HALF:N], ALU.add)
         quantize_z(1)
         product(0, 2)
         product(0, 3)
-        interleave(z2b[1], z2hi)
+        interleave(z2_bf[1], z2[1])
         quantize_z2(1)
         for t in range(R):
             product(1, t)
 
         out_v = out_0.rearrange("(p t) v -> p t v", t=R)
         words_v = out_1[0].rearrange("p n t -> p (n t)").bitcast(I32)
-        oq = sb("oq", [P, N], U32)
-        os_ = sb("os_", [P, N], U8)
-        pieces = [(0, 256), (256, 128), (384, 128)]
+        out_words = sb("out_words", [P, N], U32)
+        out_scales = sb("out_scales", [P, N], U8)
+        out_bf = [sb("out_bf%d" % i, [P, R * width], BF16) for i, (first, width) in enumerate(PIECES)]
 
-        obs = [sb("ob%d" % h, [P, R * w], BF16) for h, (c0, w) in enumerate(pieces)]
+        def hand_on(i):
+            piece = cols(*PIECES[i])
+            nc.vector.quantize_mx(
+                out=out_words[:, piece].bitcast(FP8X4), scales=out_scales[:, piece], in_=out_bf[i][:]
+            )
+            nc.sync.dma_start(words_v[:, piece], out_words[:, piece].bitcast(I32))
 
-        def hand_on(h):
-            c0, w = pieces[h]
-            ob = obs[h]
-            nc.vector.quantize_mx(out=oq[:, cols(c0, w)].bitcast(FP8X4), scales=os_[:, cols(c0, w)], in_=ob[:])
-            nc.sync.dma_start(words_v[:, cols(c0, w)], oq[:, cols(c0, w)].bitcast(I32))
-
-        for h, (c0, w) in enumerate(pieces):
-            of = sb("of%d" % h, [P, R, w], F32)
-            g4 = sb("g4_%d" % h, [P, R, w], F32)
-            g5 = sb("g5_%d" % h, [P, R, w], F32)
-            m = sb("m_%d" % h, [P, R, w], F32)
+        for i, (first, width) in enumerate(PIECES):
+            piece = cols(first, width)
+            out_f = sb("out_f%d" % i, [P, R, width], F32)
+            s_n4 = sb("s_n4_%d" % i, [P, R, width], F32)
+            s_n5 = sb("s_n5_%d" % i, [P, R, width], F32)
+            larger = sb("larger%d" % i, [P, R, width], F32)
             for t in range(R):
-                nc.scalar.activation(g4[:, t, :], s[t][:].indirect(entries(l4, c0, w)), ACT.Copy)
-                if h == 0:
-                    nc.vector.tensor_copy(g5[:, t, :], s[t][:].indirect(entries(l5, c0, w)))
+                nc.scalar.activation(s_n4[:, t, :], s[t][:].indirect(entries(l4, first, width)), ACT.Copy)
+                if t < N5_PLANES_ON_VECTOR[i]:
+                    nc.vector.tensor_copy(s_n5[:, t, :], s[t][:].indirect(entries(l5, first, width)))
                 else:
-                    nc.scalar.activation(g5[:, t, :], s[t][:].indirect(entries(l5, c0, w)), ACT.Copy)
-            nc.vector.tensor_tensor(m[:, 0:2, :], g4[:, 0:2, :], g5[:, 0:2, :], ALU.max)
-            if h > 0:
-                hand_on(h - 1)
-            nc.vector.tensor_tensor(m[:, 2:4, :], g4[:, 2:4, :], g5[:, 2:4, :], ALU.max)
-            for t in range(R):
-                nc.vector.scalar_tensor_tensor(
-                    of[:, t, :], s[t][:, cols(c0, w)], -0.75, m[:, t, :], ALU.mult, ALU.add
-                )
-            nc.sync.dma_start(out_v[:, :, cols(c0, w)], of[:])
-            interleave(obs[h], of)
-        hand_on(len(pieces) - 1)
+                    nc.scalar.activation(s_n5[:, t, :], s[t][:].indirect(entries(l5, first, width)), ACT.Copy)
+            for t0 in (0, 2):
+                pair = slice(t0, t0 + 2)
+                nc.vector.tensor_tensor(larger[:, pair, :], s_n4[:, pair, :], s_n5[:, pair, :], ALU.max)
+                if i > 0 and t0 == 0:
+                    hand_on(i - 1)
+                for t in (t0, t0 + 1):
+                    nc.vector.scalar_tensor_tensor(
+                        out_f[:, t, :], s[t][:, piece], -0.75, larger[:, t, :], ALU.mult, ALU.add
+                    )
+            nc.sync.dma_start(out_v[:, :, piece], out_f[:])
+            interleave(out_bf[i], out_f)
+        hand_on(len(PIECES) - 1)
+
         for q in range(4):
             queue = (nc.sync, nc.scalar)[q % 2]
-            queue.dma_start(out_2[0, 4 * q : 4 * q + 4, :].bitcast(I32), os_[32 * q : 32 * q + 4, :].bitcast(I32))
+            queue.dma_start(
+                out_2[0, 4 * q : 4 * q + 4, :].bitcast(I32), out_scales[QUAD * q : QUAD * q + 4, :].bitcast(I32)
+            )

from contextlib import ExitStack

import concourse.mybir as mybir

F32 = mybir.dt.float32
BF16 = mybir.dt.bfloat16
I32 = mybir.dt.int32
U32 = mybir.dt.uint32
U16 = mybir.dt.uint16
U8 = mybir.dt.uint8
FP8X4 = mybir.dt.float8_e4m3fn_x4
FP4X4 = mybir.dt.float4_e2m1fn_x4
ALU = mybir.AluOpType
ACT = mybir.ActivationFunctionType

P = 128
R = 4
N = 512
T = 2048
GROUP = 16
QUAD = 32
HALF = N // 2
PIECES = ((0, 256), (256, 128), (384, 128))
N5_PLANES_ON_VECTOR = (4, 2, 0)
FLOPS = 3 * 2 * N * N * N


def tile_picked_hkqtwicpkindgover_none_po_kernel(
    tc, x_words, x_scales, w1_words, w1_scales, w2_words, w2_scales, tab, ga, gb,
    offs, two, n1, n2, n3, n4, n5, out_0, out_1, out_2,
):
    nc = tc.nc
    with ExitStack() as ctx:
        keep = ctx.enter_context(tc.tile_pool(name="keep", bufs=1))
        psum = ctx.enter_context(tc.psum_pool(name="psum", bufs=1))

        def sb(name, shape, dtype, tag=None):
            return keep.tile(shape, dtype, name=name, tag=tag or name, align_bytes=64)

        def planes(name, width):
            return [sb("%s%d" % (name, t), [P, width], F32) for t in range(R)]

        def cols(first, width):
            return slice(first, first + width)

        def entries(list_tile, first, width):
            return list_tile[:, first // GROUP : (first + width) // GROUP]

        l_offs, l_two, l1, l2, l3, l4, l5 = [sb("list%d" % i, [P, N // GROUP], U16) for i in range(7)]
        xw = sb("xw", [P, T], U32)
        xs = sb("xs", [P, T], U8)
        w1raw = sb("w1raw", [P, 2 * N], U8)
        ws_stage = sb("ws_stage", [P, N], U8)
        tabs = planes("tab", 2 * N)

        nc.vector.memset(xs[:].bitcast(I32), 0)
        nc.vector.memset(ws_stage[:].bitcast(I32), 0)
        for t in range(R):
            nc.vector.memset(tabs[t][:, N : 2 * N], 0.0)

        tab_v = tab.rearrange("(p t) c -> p t c", t=R)

        def load_weight_scales(src):
            for r in range(4):
                nc.sync.dma_start(ws_stage[r:P:QUAD, :].bitcast(I32), src[0, r:16:4, :].bitcast(I32))

        nc.sync.dma_start(l_offs[:], offs)
        for e in range(2):
            nc.sync.dma_start(xs[e:P:GROUP, :].bitcast(I32), x_scales[0, e:16:2, :].bitcast(I32))
        nc.sync.dma_start(l2[:], n2)
        nc.sync.dma_start(tabs[0][:, 0:N], tab_v[:, 0, :])
        nc.sync.dma_start(w1raw[:].bitcast(I32), w1_words[0].bitcast(I32))
        nc.sync.dma_start(l_two[:], two)
        nc.sync.dma_start(xw[:].bitcast(I32), x_words[0].rearrange("p n t -> p (n t)").bitcast(I32))
        load_weight_scales(w1_scales)
        ga_sb = sb("ga_sb", [P, R], F32)
        nc.sync.dma_start(l1[:], n1)
        nc.sync.dma_start(tabs[1][:, 0:N], tab_v[:, 1, :])
        nc.sync.dma_start(tabs[2][:, 0:N], tab_v[:, 2, :])
        w2raw = sb("w2raw", [P, 2 * N], U8)
        nc.sync.dma_start(w2raw[:].bitcast(I32), w2_words[0].bitcast(I32))
        nc.sync.dma_start(tabs[3][:, 0:N], tab_v[:, 3, :])
        nc.sync.dma_start(ga_sb[:], ga.rearrange("(p t) o -> p (t o)", t=R))
        nc.sync.dma_start(l3[:], n3)
        nc.sync.dma_start(l4[:], n4)
        nc.sync.dma_start(l5[:], n5)

        warm = sb("warm", [P, 8], F32)
        nc.scalar.activation(warm[:, 0:1], tabs[0][:, N : N + 1], ACT.Sigmoid)

        def deal_words(name, raw):
            words = sb(name, [P, 2 * N], U8)
            nc.vector.tensor_copy(
                words[:].rearrange("p (t m b) -> p t m b", t=R, b=2),
                raw[:].rearrange("p (m t b) -> p t m b", t=R, b=2),
            )
            return words

        def deal_scales(name, tag=None):
            scales = sb(name, [P, N], U8, tag=tag)
            nc.vector.tensor_copy(
                scales[:].rearrange("p (t m) -> p t m", t=R),
                ws_stage[:].rearrange("p (m t) -> p t m", t=R),
            )
            return scales

        w1w = deal_words("w1w", w1raw)

        picked_s = sb("picked_s", [P, 2 * N], U8)
        xq_s = sb("xq_s", [P, 2 * N], U8)
        nc.vector.tensor_copy(picked_s[:, 0:N], xs[:].indirect(l_offs[:]))
        nc.vector.tensor_copy(picked_s[:, N : 2 * N], xs[:].indirect(l_two[:]))
        nc.vector.tensor_copy(xq_s[:].bitcast(I32), picked_s[:].bitcast(I32))
        for e in range(2):
            nc.sync.dma_start(
                xq_s[2 + e : P : QUAD, :].bitcast(I32), picked_s[GROUP + e : P : QUAD, :].bitcast(I32)
            )

        def project(banks_tag, words, scales, picked_words, picked_scales):
            banks = []
            for t in range(R):
                bank = psum.tile([P, N], F32, name="%s%d" % (banks_tag, t), tag="%s%d" % (banks_tag, t))
                nc.tensor.matmul_mx(
                    out=bank[:],
                    lhsT=words[:, cols(2 * P * t, 2 * P)].bitcast(FP4X4),
                    lhsT_scale=scales[:, cols(P * t, P)],
                    rhs=picked_words[:].bitcast(FP8X4),
                    rhs_scale=picked_scales,
                    start=True,
                    stop=True,
                )
                banks.append(bank)
            return banks

        sg = planes("sg", 2 * N)
        st = planes("st", 2 * N)
        tab_n2 = [sg[t][:, N : 2 * N] for t in range(R)]
        a_scaled = [st[t][:, N : 2 * N] for t in range(R)]
        for t in range(R):
            nc.scalar.activation(tab_n2[t], tabs[t][:].indirect(l2[:]), ACT.Copy)

        xa = sb("xa", [P, N], U32)
        xb = sb("xb", [P, N], U32)
        nc.vector.tensor_copy(xa[:], xw[:].indirect(l_offs[:]))
        w1s = deal_scales("w1s")
        load_weight_scales(w2_scales)
        a_ps = project("lo", w1w, w1s, xa, xq_s[:, 0:N])
        nc.vector.tensor_copy(xb[:], xw[:].indirect(l_two[:]))
        gb_sb = sb("gb_sb", [P, R], F32, tag="tab1")
        nc.sync.dma_start(gb_sb[:], gb.rearrange("(p t) o -> p (t o)", t=R))
        w2w = deal_words("w2w", w2raw)
        w2s = deal_scales("w2s", tag="xa")
        b_ps = project("hi", w2w, w2s, xb, xq_s[:, N : 2 * N])

        half_sign = sb("half_sign", [P, R], F32)
        ga_abs = sb("ga_abs", [P, R], F32)
        gb_half = sb("gb_half", [P, R], F32, tag="w1s")
        nc.vector.tensor_scalar(half_sign[:], ga_sb[:], 0.0, -0.5, ALU.is_ge, ALU.add)
        nc.vector.scalar_tensor_tensor(ga_abs[:], ga_sb[:], 2.0, half_sign[:], ALU.mult, ALU.mult)
        nc.vector.scalar_tensor_tensor(gb_half[:], gb_sb[:], -1.0, half_sign[:], ALU.mult, ALU.mult)

        for t in range(R):
            nc.scalar.activation(sg[t][:, 0:N], a_ps[t][:], ACT.Sigmoid)
            nc.scalar.activation(a_scaled[t], a_ps[t][:], ACT.Copy, scale=ga_abs[:, t : t + 1])
            nc.vector.tensor_tensor(st[t][:, 0:N], sg[t][:].indirect(l1[:]), a_scaled[t], ALU.mult)

        b_half = planes("b_half", N)
        st_n1 = planes("st_n1", N)
        b_tab = sb("b_tab", [P, R, N], F32)
        z = sb("z", [P, R, N], F32)
        z2 = [sb("z2_%d" % h, [P, R, HALF], F32) for h in range(2)]
        for t in range(R):
            nc.scalar.activation(b_half[t][:], b_ps[t][:], ACT.Copy, scale=gb_half[:, t : t + 1])
            nc.scalar.activation(st_n1[t][:], st[t][:].indirect(l1[:]), ACT.Copy)
            nc.vector.scalar_tensor_tensor(b_tab[:, t, :], b_half[t][:], -2.0, tab_n2[t], ALU.mult, ALU.mult)
            nc.vector.tensor_tensor(
                z2[0][:, t, :], b_half[t][:].indirect(entries(l3, 0, HALF)), b_tab[:, t, 0:HALF], ALU.add
            )
            nc.vector.tensor_tensor(z[:, t, :], st[t][:, 0:N], st_n1[t][:], ALU.max)

        b_n3 = sb("b_n3", [P, R, HALF], F32)
        for t in range(R):
            nc.scalar.activation(b_n3[:, t, :], b_half[t][:].indirect(entries(l3, HALF, HALF)), ACT.Copy)

        z_bf = sb("z_bf", [P, R * N], BF16)
        z_words = sb("z_words", [P, N], U32)
        z_scales = sb("z_scales", [P, N], U8)
        z2_bf = [sb("z2_bf%d" % h, [P, R * HALF], BF16) for h in range(2)]
        z2_words = [sb("z2_words%d" % h, [P, HALF], U32) for h in range(2)]
        z2_scales = [sb("z2_scales%d" % h, [P, HALF], U8) for h in range(2)]

        def interleave(dst, src):
            nc.vector.tensor_copy(
                dst[:].rearrange("p (c i k) -> p c k i", i=4, k=R),
                src[:].rearrange("p k (c i) -> p c k i", i=4),
            )

        def quantize_z(g):
            nc.vector.quantize_mx(
                out=z_words[:, cols(2 * P * g, 2 * P)].bitcast(FP8X4),
                scales=z_scales[:, cols(2 * P * g, 2 * P)],
                in_=z_bf[:, cols(2 * P * R * g, 2 * P * R)],
            )

        def quantize_z2(h):
            nc.vector.quantize_mx(out=z2_words[h][:].bitcast(FP8X4), scales=z2_scales[h][:], in_=z2_bf[h][:])

        s = planes("s", N)

        def product(h, t):
            banks_tag = "%s%d" % (("lo", "hi")[h], t)
            bank = psum.tile([P, N], F32, name="s" + banks_tag, tag=banks_tag)
            nc.tensor.matmul_mx(
                out=bank[:, 0:HALF],
                lhsT=z_words[:, cols(P * t, P)].bitcast(FP8X4),
                lhsT_scale=z_scales[:, cols(P * t, P)],
                rhs=z2_words[h][:].bitcast(FP8X4),
                rhs_scale=z2_scales[h][:],
                start=True,
                stop=True,
            )
            nc.scalar.activation(s[t][:, cols(h * HALF, HALF)], bank[:, 0:HALF], ACT.Copy, scale=0.0625)

        interleave(z2_bf[0], z2[0])
        nc.vector.tensor_copy(
            z_bf[:].rearrange("p (g e m k) -> p g m k e", g=2, e=2, k=R),
            z[:].rearrange("p k (m g e) -> p g m k e", g=2, e=2),
        )
        quantize_z2(0)
        quantize_z(0)
        product(0, 0)
        product(0, 1)
        nc.vector.tensor_tensor(z2[1][:], b_n3[:], b_tab[:, :, HALF:N], ALU.add)
        quantize_z(1)
        product(0, 2)
        product(0, 3)
        interleave(z2_bf[1], z2[1])
        quantize_z2(1)
        for t in range(R):
            product(1, t)

        out_v = out_0.rearrange("(p t) v -> p t v", t=R)
        words_v = out_1[0].rearrange("p n t -> p (n t)").bitcast(I32)
        out_words = sb("out_words", [P, N], U32)
        out_scales = sb("out_scales", [P, N], U8)
        out_bf = [sb("out_bf%d" % i, [P, R * width], BF16) for i, (first, width) in enumerate(PIECES)]

        def hand_on(i):
            piece = cols(*PIECES[i])
            nc.vector.quantize_mx(
                out=out_words[:, piece].bitcast(FP8X4), scales=out_scales[:, piece], in_=out_bf[i][:]
            )
            nc.sync.dma_start(words_v[:, piece], out_words[:, piece].bitcast(I32))

        for i, (first, width) in enumerate(PIECES):
            piece = cols(first, width)
            out_f = sb("out_f%d" % i, [P, R, width], F32)
            s_n4 = sb("s_n4_%d" % i, [P, R, width], F32)
            s_n5 = sb("s_n5_%d" % i, [P, R, width], F32)
            larger = sb("larger%d" % i, [P, R, width], F32)
            for t in range(R):
                nc.scalar.activation(s_n4[:, t, :], s[t][:].indirect(entries(l4, first, width)), ACT.Copy)
                if t < N5_PLANES_ON_VECTOR[i]:
                    nc.vector.tensor_copy(s_n5[:, t, :], s[t][:].indirect(entries(l5, first, width)))
                else:
                    nc.scalar.activation(s_n5[:, t, :], s[t][:].indirect(entries(l5, first, width)), ACT.Copy)
            for t0 in (0, 2):
                pair = slice(t0, t0 + 2)
                nc.vector.tensor_tensor(larger[:, pair, :], s_n4[:, pair, :], s_n5[:, pair, :], ALU.max)
                if i > 0 and t0 == 0:
                    hand_on(i - 1)
                for t in (t0, t0 + 1):
                    nc.vector.scalar_tensor_tensor(
                        out_f[:, t, :], s[t][:, piece], -0.75, larger[:, t, :], ALU.mult, ALU.add
                    )
            nc.sync.dma_start(out_v[:, :, piece], out_f[:])
            interleave(out_bf[i], out_f)
        hand_on(len(PIECES) - 1)

        for q in range(4):
            queue = (nc.sync, nc.scalar)[q % 2]
            queue.dma_start(
                out_2[0, 4 * q : 4 * q + 4, :].bitcast(I32), out_scales[QUAD * q : QUAD * q + 4, :].bitcast(I32)
            )
